import numpy as np
import ml_dtypes


def mxq(x, axis, fmt="e4m3"):
    dtype, down = {"e4m3": (ml_dtypes.float8_e4m3fn, 7), "e5m2": (ml_dtypes.float8_e5m2, 14)}[fmt]
    v = np.moveaxis(np.asarray(x, np.float32).astype(ml_dtypes.bfloat16).astype(np.float64), axis, -1)
    blocks = v.reshape(v.shape[:-1] + (-1, 32))
    amax = np.abs(blocks).max(-1, keepdims=True)
    byte = np.maximum(np.where(amax > 0, np.frexp(amax)[1] - 1 + 127, 0) - down, 1)
    scale = np.exp2(byte - 127.0)
    codes = (blocks / scale).astype(np.float32).astype(dtype).astype(np.float64)
    return np.moveaxis((codes * scale).reshape(v.shape), -1, axis)


WIDE = False


def mx_kscale(k):
    if not WIDE:
        return np.ones(k)
    levels = np.array([10, -10, 5, -5, 0])
    if k % 512:
        return np.exp2(np.random.permutation(np.resize(levels, k // 32))).repeat(32)
    a = np.empty((k // 512, 16))
    for p in range(k // 512):
        a[p, :8] = np.random.permutation(np.resize(levels, 8))
        for g in range(8):
            far = levels[np.abs(levels - a[p, g]) >= 10]
            a[p, g + 8] = far[np.random.randint(len(far))]
    return np.exp2(a.ravel()).repeat(32)


def f64(x):
    return np.asarray(x).astype(np.float64)


E2M1 = np.array([0.0, 0.5, 1.0, 1.5, 2.0, 3.0, 4.0, 6.0, -0.0, -0.5, -1.0, -1.5, -2.0, -3.0, -4.0, -6.0])


def pack_weight(w, fmt):
    k, n = w.shape
    w = f64(np.asarray(w, np.float32).astype(ml_dtypes.bfloat16)).reshape(k // 32, 32, n)
    amax = np.abs(w).max(1)
    if fmt == "e4m3":
        byte = np.frexp(amax)[1] - 1 + 127 - 7
    else:
        mant, ex = np.frexp(amax / 6.0)
        byte = np.where(mant > 0.5, ex, ex - 1) + 127
    byte = np.clip(np.where(amax > 0, byte, 1), 1, 254)
    scaled = (w * np.exp2(127.0 - byte)[:, None, :]).reshape(k, n).astype(np.float32)
    by_word = np.ascontiguousarray(scaled.reshape(k // 512, 128, 4, n).transpose(0, 1, 3, 2))
    if fmt == "e4m3":
        words = by_word.astype(ml_dtypes.float8_e4m3fn).view(np.uint8)
    else:
        c = by_word.astype(ml_dtypes.float4_e2m1fn).view(np.uint8) & 0xF
        words = (c[..., 0::2] | (c[..., 1::2] << 4)).reshape(k // 512, 128, 2 * n)
    return np.ascontiguousarray(words), np.ascontiguousarray(byte.astype(np.uint8).reshape(k // 512, 16, n))


def unpack_weight(words, scales, fmt):
    g, _, n = scales.shape
    words = np.ascontiguousarray(words).reshape(g, 128, n, -1)
    if fmt == "e4m3":
        vals = words.view(ml_dtypes.float8_e4m3fn).astype(np.float64)
    else:
        nib = np.empty((g, 128, n, 4), np.uint8)
        nib[..., 0::2] = words & 0xF
        nib[..., 1::2] = words >> 4
        vals = E2M1[nib]
    vals = vals * np.repeat(np.exp2(scales.astype(np.float64) - 127.0), 8, axis=1)[..., None]
    return vals.transpose(0, 1, 3, 2).reshape(g * 512, n)


def gelu(v):
    return 0.5 * v * (1.0 + np.tanh(np.sqrt(2.0 / np.pi) * (v + 0.044715 * v**3)))


K, M, T = 512, 1536, 1536


def setup_inputs():
    n = np.random.standard_normal
    s = mx_kscale(K)[:, None]
    x = n((K, T)) * s
    x4 = pack_weight(x, "e2m1")
    rest = x - unpack_weight(*x4, "e2m1")
    p_w4 = pack_weight(n((K, M)) / np.sqrt(K) / s, "e2m1")
    return {
        "x4_words": x4[0],
        "x4_scales": x4[1],
        "xr": (rest).astype(np.float32),
        "w4_words": p_w4[0],
        "w4_scales": p_w4[1],
        "b": (0.3 * n(1536)).astype(np.float32),
    }


def reference(x4_words, x4_scales, xr, w4_words, w4_scales, b):
    x4_ = unpack_weight(x4_words, x4_scales, "e2m1")
    xr_ = mxq(f64(xr), 0, "e4m3")
    w4_ = unpack_weight(w4_words, w4_scales, "e2m1")
    y = x4_.T @ w4_ + xr_.T @ w4_
    return gelu(y + f64(b)[None, :])

@@ -1,0 +1,167 @@
+from contextlib import ExitStack
+
+import concourse.mybir as mybir
+from concourse.masks import make_identity
+
+K, M, T = 512, 1536, 1536
+FLOPS = 2 * 2 * K * M * T
+
+F32 = mybir.dt.float32
+BF16 = mybir.dt.bfloat16
+I32 = mybir.dt.int32
+U32 = mybir.dt.uint32
+U8 = mybir.dt.uint8
+E4M3X4 = mybir.dt.float8_e4m3fn_x4
+E2M1X4 = mybir.dt.float4_e2m1fn_x4
+ACT = mybir.ActivationFunctionType
+ALU = mybir.AluOpType
+
+P = 128
+NB = 512
+N_T = T // P
+N_N = M // NB
+LEAD = 5
+CHUNKS = [(0, 256), (256, 512), (768, 768)]
+
+
+def tile_mix_xres_tm_gelu_kernel(tc, x4_words, x4_scales, xr, w4_words, w4_scales, b, out):
+    nc = tc.nc
+    with ExitStack() as ctx:
+        keep = ctx.enter_context(tc.tile_pool(name="keep", bufs=1))
+        pre = ctx.enter_context(tc.tile_pool(name="pre", bufs=3))
+        post = ctx.enter_context(tc.tile_pool(name="post", bufs=5))
+        psum = ctx.enter_context(tc.psum_pool(name="psum", bufs=8))
+        ctx.enter_context(tc.manual_schedule())
+
+        w_words = keep.tile([P, 2 * M], U8, name="w_words", align_bytes=256)
+        w_sc = keep.tile([P, M], U8, name="w_sc", align_bytes=256)
+        x_words = keep.tile([P, 2 * T], U8, name="x_words", align_bytes=256)
+        x_sc = keep.tile([P, T], U8, name="x_sc", align_bytes=256)
+        b_rows = keep.tile([P, 3, P], F32, name="b_rows")
+        b_cols = keep.tile([P, 12], F32, name="b_cols")
+        bias = keep.tile([P, M], F32, name="bias", align_bytes=256)
+        ident = keep.tile([P, P], F32, name="ident")
+        warm = keep.tile([P, 1], F32, name="warm")
+        warm_out = keep.tile([P, 1], F32, name="warm_out")
+        raw = [keep.tile([P, 4, w], F32, name="raw%d" % i, align_bytes=256) for i, (c, w) in enumerate(CHUNKS)]
+        grouped = [keep.tile([P, P, 4], BF16, name="grp%d" % i, align_bytes=256) for i in range(N_T)]
+        codes = [keep.tile([P, P], U32, name="codes%d" % i, align_bytes=256) for i in range(N_T)]
+        scales = [keep.tile([P, P], U8, name="scl%d" % i, align_bytes=64) for i in range(N_T)]
+
+        nc.vector.memset(b_rows[:], 0.0)
+        nc.vector.memset(w_sc[:].bitcast(I32), 0)
+        nc.vector.memset(x_sc[:].bitcast(I32), 0)
+        nc.vector.memset(warm[:], 0.0)
+        make_identity(nc, ident[:])
+        nc.scalar.dma_start(out=b_rows[0:4].rearrange("r j c -> r (j c)"), in_=b.rearrange("(r c) -> r c", r=4))
+
+        def scale_dma(eng, dst, src, q):
+            eng.dma_start(out=dst[32 * q : 32 * q + 4, :].bitcast(I32), in_=src[0][4 * q : 4 * q + 4, :].bitcast(I32))
+
+        for q in range(4):
+            scale_dma(nc.scalar, w_sc, w4_scales, q)
+        nc.sync.dma_start(out=w_words[:].bitcast(I32), in_=w4_words[0].bitcast(I32))
+        nc.sync.dma_start(out=x_words[:].bitcast(I32), in_=x4_words[0].bitcast(I32))
+        scale_dma(nc.gpsimd, x_sc, x4_scales, 0)
+        scale_dma(nc.gpsimd, x_sc, x4_scales, 1)
+        xr_rows = xr.rearrange("(p j) t -> p j t", j=4)
+        nc.sync.dma_start(out=raw[0][:], in_=xr_rows[:, :, 0:256])
+        scale_dma(nc.scalar, x_sc, x4_scales, 2)
+        scale_dma(nc.scalar, x_sc, x4_scales, 3)
+        for r, (c, w) in list(zip(raw, CHUNKS))[1:]:
+            nc.sync.dma_start(out=r[:], in_=xr_rows[:, :, c : c + w])
+        nc.scalar.activation(out=warm_out[:], in_=warm[:], func=ACT.Gelu_apprx_tanh)
+
+        turned = psum.tile([P, 3, P], F32, name="turned", tag="acc")
+        for j in range(3):
+            nc.tensor.transpose(turned[:, j, :], b_rows[:, j, :], ident[:])
+        nc.vector.tensor_copy(
+            out=b_cols[:].rearrange("p (r j) -> p r j", j=3), in_=turned[:, :, 0:4].rearrange("p j r -> p r j")
+        )
+        for n in range(N_N):
+            spread = psum.tile([P, NB], F32, name="spread", tag="acc")
+            for i in range(4):
+                c = 4 * n + i
+                nc.tensor.transpose(spread[:, i * P : (i + 1) * P], b_cols[:, c : c + 1].to_broadcast([P, P]), ident[:])
+            nc.scalar.copy(out=bias[:, n * NB : (n + 1) * NB], in_=spread[:])
+
+        def views(i, lo, hi):
+            t0 = i * P
+            r, c = [(r, c) for r, (c, w) in zip(raw, CHUNKS) if c <= t0 < c + w][0]
+            src = r[:, :, t0 - c + lo : t0 - c + hi].rearrange("p j (c i) -> p c j i", i=4)
+            dst = grouped[i][:, lo:hi, :].rearrange("p (c i) j -> p c j i", i=4)
+            return dst, src
+
+        def copy_v(i, lo, hi):
+            dst, src = views(i, lo, hi)
+            nc.vector.tensor_copy(out=dst, in_=src)
+
+        def copy_s(i, lo, hi):
+            dst, src = views(i, lo, hi)
+            nc.scalar.copy(out=dst, in_=src)
+
+        def copy_g(i, lo, hi):
+            dst, src = views(i, lo, hi)
+            nc.gpsimd.tensor_scalar(out=dst, in0=src, scalar1=1.0, scalar2=0.0, op0=ALU.mult, op1=ALU.add)
+
+        def quantize(i):
+            nc.vector.quantize_mx(
+                out=codes[i][:].bitcast(E4M3X4), scales=scales[i][:], in_=grouped[i][:].rearrange("p t j -> p (t j)")
+            )
+
+        groups = [(i, n) for i in range(N_T) for n in range(N_N)]
+        acc = {}
+
+        def pass_x4(g):
+            i, n = groups[g]
+            bank = psum.tile([P, NB], F32, name="bank", tag="acc")
+            acc[g] = bank
+            nc.tensor.matmul_mx(
+                out=bank[:],
+                lhsT=x_words[:, 2 * P * i : 2 * P * (i + 1)].bitcast(E2M1X4),
+                lhsT_scale=x_sc[:, P * i : P * (i + 1)],
+                rhs=w_words[:, 2 * NB * n : 2 * NB * (n + 1)].bitcast(E2M1X4),
+                rhs_scale=w_sc[:, NB * n : NB * (n + 1)],
+                start=True,
+                stop=False,
+            )
+
+        def pass_xr(g):
+            i, n = groups[g]
+            nc.tensor.matmul_mx(
+                out=acc[g][:],
+                lhsT=codes[i][:].bitcast(E4M3X4),
+                lhsT_scale=scales[i][:],
+                rhs=w_words[:, 2 * NB * n : 2 * NB * (n + 1)].bitcast(E2M1X4),
+                rhs_scale=w_sc[:, NB * n : NB * (n + 1)],
+                start=False,
+                stop=True,
+            )
+
+        for i in range(2):
+            copy_s(i, 80, 128)
+            copy_v(i, 0, 80)
+        for i in range(2):
+            quantize(i)
+        for i in range(2, N_T):
+            copy_g(i, 0, 128)
+        for g in range(LEAD):
+            pass_x4(g)
+
+        for i in range(N_T):
+            pre_t = pre.tile([P, M], F32, name="pre_t", align_bytes=64)
+            res = post.tile([P, M], F32, name="res", align_bytes=64)
+            for n in range(N_N):
+                g = N_N * i + n
+                if g + LEAD < len(groups):
+                    pass_x4(g + LEAD)
+                pass_xr(g)
+                cols = slice(n * NB, (n + 1) * NB)
+                nc.vector.tensor_add(out=pre_t[:, cols], in0=acc[g][:], in1=bias[:, cols])
+                if n == 0 and 2 <= i + 1 < N_T:
+                    quantize(i + 1)
+                nc.scalar.activation(out=res[:, cols], in_=pre_t[:, cols], func=ACT.Gelu_apprx_tanh)
+                if i == N_T - 1:
+                    nc.sync.dma_start(out=out[i * P : (i + 1) * P, cols], in_=res[:, cols])
+            if i < N_T - 1:
+                nc.sync.dma_start(out=out[i * P : (i + 1) * P, :], in_=res[:])

@@ -1,7 +1,6 @@
 from contextlib import ExitStack
 
 import concourse.mybir as mybir
-from concourse.masks import make_identity
 
 K, M, T = 512, 1536, 1536
 FLOPS = 2 * 2 * K * M * T
@@ -20,7 +19,8 @@ P = 128
 NB = 512
 N_T = T // P
 N_N = M // NB
-LEAD = 5
+LEAD = 3
+V_COLS = 72
 CHUNKS = [(0, 256), (256, 512), (768, 768)]
 
 
@@ -37,10 +37,10 @@ def tile_mix_xres_tm_gelu_kernel(tc, x4_words, x4_scales, xr, w4_words, w4_scale
         w_sc = keep.tile([P, M], U8, name="w_sc", align_bytes=256)
         x_words = keep.tile([P, 2 * T], U8, name="x_words", align_bytes=256)
         x_sc = keep.tile([P, T], U8, name="x_sc", align_bytes=256)
-        b_rows = keep.tile([P, 3, P], F32, name="b_rows")
-        b_cols = keep.tile([P, 12], F32, name="b_cols")
+        b_rows = keep.tile([P, P], F32, name="b_rows", align_bytes=64)
+        b_cols = keep.tile([P, P], F32, name="b_cols", align_bytes=64)
+        b_wide = [keep.tile([P, 16, 32], F32, name="b_wide%d" % n, align_bytes=64) for n in range(N_N)]
         bias = keep.tile([P, M], F32, name="bias", align_bytes=256)
-        ident = keep.tile([P, P], F32, name="ident")
         warm = keep.tile([P, 1], F32, name="warm")
         warm_out = keep.tile([P, 1], F32, name="warm_out")
         raw = [keep.tile([P, 4, w], F32, name="raw%d" % i, align_bytes=256) for i, (c, w) in enumerate(CHUNKS)]
@@ -48,42 +48,32 @@ def tile_mix_xres_tm_gelu_kernel(tc, x4_words, x4_scales, xr, w4_words, w4_scale
         codes = [keep.tile([P, P], U32, name="codes%d" % i, align_bytes=256) for i in range(N_T)]
         scales = [keep.tile([P, P], U8, name="scl%d" % i, align_bytes=64) for i in range(N_T)]
 
-        nc.vector.memset(b_rows[:], 0.0)
         nc.vector.memset(w_sc[:].bitcast(I32), 0)
         nc.vector.memset(x_sc[:].bitcast(I32), 0)
         nc.vector.memset(warm[:], 0.0)
-        make_identity(nc, ident[:])
-        nc.scalar.dma_start(out=b_rows[0:4].rearrange("r j c -> r (j c)"), in_=b.rearrange("(r c) -> r c", r=4))
+        nc.vector.memset(b_rows[:], 0.0)
 
         def scale_dma(eng, dst, src, q):
             eng.dma_start(out=dst[32 * q : 32 * q + 4, :].bitcast(I32), in_=src[0][4 * q : 4 * q + 4, :].bitcast(I32))
 
+        xr_rows = xr.rearrange("(p j) t -> p j t", j=4)
+        b_view = b.rearrange("(w j c) -> j w c", w=3, c=32)
+        nc.sync.dma_start(out=raw[0][:], in_=xr_rows[:, :, 0:256])
+        nc.gpsimd.dma_start(out=x_words[:].bitcast(I32), in_=x4_words[0].bitcast(I32))
+        nc.sync.dma_start(out=w_words[:].bitcast(I32), in_=w4_words[0].bitcast(I32))
         for q in range(4):
             scale_dma(nc.scalar, w_sc, w4_scales, q)
-        nc.sync.dma_start(out=w_words[:].bitcast(I32), in_=w4_words[0].bitcast(I32))
-        nc.sync.dma_start(out=x_words[:].bitcast(I32), in_=x4_words[0].bitcast(I32))
-        scale_dma(nc.gpsimd, x_sc, x4_scales, 0)
-        scale_dma(nc.gpsimd, x_sc, x4_scales, 1)
-        xr_rows = xr.rearrange("(p j) t -> p j t", j=4)
-        nc.sync.dma_start(out=raw[0][:], in_=xr_rows[:, :, 0:256])
-        scale_dma(nc.scalar, x_sc, x4_scales, 2)
-        scale_dma(nc.scalar, x_sc, x4_scales, 3)
+        scale_dma(nc.scalar, x_sc, x4_scales, 0)
+        scale_dma(nc.scalar, x_sc, x4_scales, 1)
+        scale_dma(nc.gpsimd, x_sc, x4_scales, 2)
+        scale_dma(nc.gpsimd, x_sc, x4_scales, 3)
+        nc.scalar.activation(out=warm_out[:], in_=warm[:], func=ACT.Gelu_apprx_tanh)
+        for q in range(4):
+            nc.scalar.dma_start(
+                out=b_rows[32 * q : 32 * q + 16, 0:96].rearrange("j (w c) -> j w c", w=3), in_=b_view
+            )
         for r, (c, w) in list(zip(raw, CHUNKS))[1:]:
             nc.sync.dma_start(out=r[:], in_=xr_rows[:, :, c : c + w])
-        nc.scalar.activation(out=warm_out[:], in_=warm[:], func=ACT.Gelu_apprx_tanh)
-
-        turned = psum.tile([P, 3, P], F32, name="turned", tag="acc")
-        for j in range(3):
-            nc.tensor.transpose(turned[:, j, :], b_rows[:, j, :], ident[:])
-        nc.vector.tensor_copy(
-            out=b_cols[:].rearrange("p (r j) -> p r j", j=3), in_=turned[:, :, 0:4].rearrange("p j r -> p r j")
-        )
-        for n in range(N_N):
-            spread = psum.tile([P, NB], F32, name="spread", tag="acc")
-            for i in range(4):
-                c = 4 * n + i
-                nc.tensor.transpose(spread[:, i * P : (i + 1) * P], b_cols[:, c : c + 1].to_broadcast([P, P]), ident[:])
-            nc.scalar.copy(out=bias[:, n * NB : (n + 1) * NB], in_=spread[:])
 
         def views(i, lo, hi):
             t0 = i * P
@@ -100,10 +90,6 @@ def tile_mix_xres_tm_gelu_kernel(tc, x4_words, x4_scales, xr, w4_words, w4_scale
             dst, src = views(i, lo, hi)
             nc.scalar.copy(out=dst, in_=src)
 
-        def copy_g(i, lo, hi):
-            dst, src = views(i, lo, hi)
-            nc.gpsimd.tensor_scalar(out=dst, in0=src, scalar1=1.0, scalar2=0.0, op0=ALU.mult, op1=ALU.add)
-
         def quantize(i):
             nc.vector.quantize_mx(
                 out=codes[i][:].bitcast(E4M3X4), scales=scales[i][:], in_=grouped[i][:].rearrange("p t j -> p (t j)")
@@ -112,30 +98,45 @@ def tile_mix_xres_tm_gelu_kernel(tc, x4_words, x4_scales, xr, w4_words, w4_scale
         groups = [(i, n) for i in range(N_T) for n in range(N_N)]
         acc = {}
 
+        def open_bank(g):
+            first = g not in acc
+            if first:
+                bank = psum.tile([P, NB], F32, name="bank", tag="acc")
+                acc[g] = bank
+            return first
+
         def pass_x4(g):
             i, n = groups[g]
-            bank = psum.tile([P, NB], F32, name="bank", tag="acc")
-            acc[g] = bank
+            first = open_bank(g)
             nc.tensor.matmul_mx(
-                out=bank[:],
+                out=acc[g][:],
                 lhsT=x_words[:, 2 * P * i : 2 * P * (i + 1)].bitcast(E2M1X4),
                 lhsT_scale=x_sc[:, P * i : P * (i + 1)],
                 rhs=w_words[:, 2 * NB * n : 2 * NB * (n + 1)].bitcast(E2M1X4),
                 rhs_scale=w_sc[:, NB * n : NB * (n + 1)],
-                start=True,
-                stop=False,
+                start=first,
+                stop=not first,
             )
 
         def pass_xr(g):
             i, n = groups[g]
+            first = open_bank(g)
             nc.tensor.matmul_mx(
                 out=acc[g][:],
                 lhsT=codes[i][:].bitcast(E4M3X4),
                 lhsT_scale=scales[i][:],
                 rhs=w_words[:, 2 * NB * n : 2 * NB * (n + 1)].bitcast(E2M1X4),
                 rhs_scale=w_sc[:, NB * n : NB * (n + 1)],
-                start=False,
-                stop=True,
+                start=first,
+                stop=not first,
+            )
+
+        def widen(copy, n):
+            copy(out=b_wide[n][:], in_=b_cols[:, 32 * n : 32 * n + 16].unsqueeze(2).to_broadcast([P, 16, 32]))
+
+        def turn(n):
+            nc.vector.transpose(
+                out=bias[:, n * NB : (n + 1) * NB], in_=b_wide[n][:].rearrange("p j a -> p (j a)")
             )
 
         for i in range(2):
@@ -143,24 +144,43 @@ def tile_mix_xres_tm_gelu_kernel(tc, x4_words, x4_scales, xr, w4_words, w4_scale
             copy_v(i, 0, 80)
         for i in range(2):
             quantize(i)
-        for i in range(2, N_T):
-            copy_g(i, 0, 128)
-        for g in range(LEAD):
-            pass_x4(g)
+        nc.vector.transpose(out=b_cols[:], in_=b_rows[:])
+        widen(nc.vector.tensor_copy, 0)
+        widen(nc.scalar.copy, 1)
+        widen(nc.scalar.copy, 2)
+        turn(0)
+        pass_xr(0)
+        pass_xr(1)
+        pass_x4(0)
+        pass_x4(1)
+        pass_xr(2)
+        pass_x4(2)
+
+        copy_slot = {2: (0, 1), 3: (0, 2)}
+        for j in range(4, N_T):
+            copy_slot[j] = (j - 3, 1)
+        quant_slot = {j: (j - 1, 0) for j in range(2, N_T)}
 
         for i in range(N_T):
             pre_t = pre.tile([P, M], F32, name="pre_t", align_bytes=64)
             res = post.tile([P, M], F32, name="res", align_bytes=64)
             for n in range(N_N):
                 g = N_N * i + n
+                if i > 0:
+                    pass_xr(g)
                 if g + LEAD < len(groups):
                     pass_x4(g + LEAD)
-                pass_xr(g)
                 cols = slice(n * NB, (n + 1) * NB)
+                if i == 0 and n > 0:
+                    turn(n)
                 nc.vector.tensor_add(out=pre_t[:, cols], in0=acc[g][:], in1=bias[:, cols])
-                if n == 0 and 2 <= i + 1 < N_T:
-                    quantize(i + 1)
                 nc.scalar.activation(out=res[:, cols], in_=pre_t[:, cols], func=ACT.Gelu_apprx_tanh)
+                for j in range(2, N_T):
+                    if copy_slot[j] == (i, n):
+                        copy_v(j, 0, V_COLS)
+                        copy_s(j, V_COLS, P)
+                    if quant_slot[j] == (i, n):
+                        quantize(j)
                 if i == N_T - 1:
                     nc.sync.dma_start(out=out[i * P : (i + 1) * P, cols], in_=res[:, cols])
             if i < N_T - 1:

@@ -20,7 +20,6 @@ NB = 512
 N_T = T // P
 N_N = M // NB
 LEAD = 3
-V_COLS = 72
 CHUNKS = [(0, 256), (256, 512), (768, 768)]
 
 
@@ -37,41 +36,38 @@ def tile_mix_xres_tm_gelu_kernel(tc, x4_words, x4_scales, xr, w4_words, w4_scale
         w_sc = keep.tile([P, M], U8, name="w_sc", align_bytes=256)
         x_words = keep.tile([P, 2 * T], U8, name="x_words", align_bytes=256)
         x_sc = keep.tile([P, T], U8, name="x_sc", align_bytes=256)
-        b_rows = keep.tile([P, P], F32, name="b_rows", align_bytes=64)
-        b_cols = keep.tile([P, P], F32, name="b_cols", align_bytes=64)
-        b_wide = [keep.tile([P, 16, 32], F32, name="b_wide%d" % n, align_bytes=64) for n in range(N_N)]
+        b_slots = keep.tile([P, N_N, 4], F32, name="b_slots", align_bytes=64)
+        b_wide = [keep.tile([P, 4, P], F32, name="b_wide%d" % n, align_bytes=64) for n in range(N_N)]
+        ident = keep.tile([P, P], F32, name="ident")
         bias = keep.tile([P, M], F32, name="bias", align_bytes=256)
         warm = keep.tile([P, 1], F32, name="warm")
         warm_out = keep.tile([P, 1], F32, name="warm_out")
         raw = [keep.tile([P, 4, w], F32, name="raw%d" % i, align_bytes=256) for i, (c, w) in enumerate(CHUNKS)]
-        grouped = [keep.tile([P, P, 4], BF16, name="grp%d" % i, align_bytes=256) for i in range(N_T)]
-        codes = [keep.tile([P, P], U32, name="codes%d" % i, align_bytes=256) for i in range(N_T)]
-        scales = [keep.tile([P, P], U8, name="scl%d" % i, align_bytes=64) for i in range(N_T)]
+        grouped = [keep.tile([P, 2 * P, 4], BF16, name="grp%d" % i, align_bytes=256) for i in range(N_T // 2)]
+        codes = [keep.tile([P, 2 * P], U32, name="codes%d" % i, align_bytes=256) for i in range(N_T // 2)]
+        scales = [keep.tile([P, 2 * P], U8, name="scl%d" % i, align_bytes=64) for i in range(N_T // 2)]
 
         nc.vector.memset(w_sc[:].bitcast(I32), 0)
         nc.vector.memset(x_sc[:].bitcast(I32), 0)
         nc.vector.memset(warm[:], 0.0)
-        nc.vector.memset(b_rows[:], 0.0)
+        nc.vector.memset(ident[:], 0.0)
+        nc.gpsimd.affine_select(
+            out=ident[:], in_=ident[:], compare_op=ALU.not_equal, fill=1.0, base=0, pattern=[[-1, P]], channel_multiplier=1
+        )
 
         def scale_dma(eng, dst, src, q):
             eng.dma_start(out=dst[32 * q : 32 * q + 4, :].bitcast(I32), in_=src[0][4 * q : 4 * q + 4, :].bitcast(I32))
 
         xr_rows = xr.rearrange("(p j) t -> p j t", j=4)
-        b_view = b.rearrange("(w j c) -> j w c", w=3, c=32)
-        nc.sync.dma_start(out=raw[0][:], in_=xr_rows[:, :, 0:256])
-        nc.gpsimd.dma_start(out=x_words[:].bitcast(I32), in_=x4_words[0].bitcast(I32))
-        nc.sync.dma_start(out=w_words[:].bitcast(I32), in_=w4_words[0].bitcast(I32))
+        nc.scalar.dma_start(out=b_slots[:], in_=b.rearrange("(w p c) -> p w c", w=N_N, c=4))
         for q in range(4):
             scale_dma(nc.scalar, w_sc, w4_scales, q)
-        scale_dma(nc.scalar, x_sc, x4_scales, 0)
-        scale_dma(nc.scalar, x_sc, x4_scales, 1)
-        scale_dma(nc.gpsimd, x_sc, x4_scales, 2)
-        scale_dma(nc.gpsimd, x_sc, x4_scales, 3)
         nc.scalar.activation(out=warm_out[:], in_=warm[:], func=ACT.Gelu_apprx_tanh)
+        nc.sync.dma_start(out=raw[0][:], in_=xr_rows[:, :, 0:256])
+        nc.sync.dma_start(out=w_words[:].bitcast(I32), in_=w4_words[0].bitcast(I32))
+        nc.sync.dma_start(out=x_words[:].bitcast(I32), in_=x4_words[0].bitcast(I32))
         for q in range(4):
-            nc.scalar.dma_start(
-                out=b_rows[32 * q : 32 * q + 16, 0:96].rearrange("j (w c) -> j w c", w=3), in_=b_view
-            )
+            scale_dma(nc.sync, x_sc, x4_scales, q)
         for r, (c, w) in list(zip(raw, CHUNKS))[1:]:
             nc.sync.dma_start(out=r[:], in_=xr_rows[:, :, c : c + w])
 
@@ -79,20 +75,27 @@ def tile_mix_xres_tm_gelu_kernel(tc, x4_words, x4_scales, xr, w4_words, w4_scale
             t0 = i * P
             r, c = [(r, c) for r, (c, w) in zip(raw, CHUNKS) if c <= t0 < c + w][0]
             src = r[:, :, t0 - c + lo : t0 - c + hi].rearrange("p j (c i) -> p c j i", i=4)
-            dst = grouped[i][:, lo:hi, :].rearrange("p (c i) j -> p c j i", i=4)
+            h = i % 2 * P
+            dst = grouped[i // 2][:, h + lo : h + hi, :].rearrange("p (c i) j -> p c j i", i=4)
             return dst, src
 
         def copy_v(i, lo, hi):
             dst, src = views(i, lo, hi)
             nc.vector.tensor_copy(out=dst, in_=src)
 
-        def copy_s(i, lo, hi):
-            dst, src = views(i, lo, hi)
-            nc.scalar.copy(out=dst, in_=src)
+        def copy_g(i, lo, hi):
+            t0 = i * P
+            r, c = [(r, c) for r, (c, w) in zip(raw, CHUNKS) if c <= t0 < c + w][0]
+            src = r[:, :, t0 - c + lo : t0 - c + hi].rearrange("p j t -> p t j")
+            nc.gpsimd.tensor_scalar(
+                out=grouped[i // 2][:, i % 2 * P + lo : i % 2 * P + hi, :], in0=src, scalar1=1.0, scalar2=0.0, op0=ALU.mult, op1=ALU.add
+            )
 
-        def quantize(i):
+        def quantize(k, lo=0, hi=2 * P):
             nc.vector.quantize_mx(
-                out=codes[i][:].bitcast(E4M3X4), scales=scales[i][:], in_=grouped[i][:].rearrange("p t j -> p (t j)")
+                out=codes[k][:, lo:hi].bitcast(E4M3X4),
+                scales=scales[k][:, lo:hi],
+                in_=grouped[k][:, lo:hi, :].rearrange("p t j -> p (t j)"),
             )
 
         groups = [(i, n) for i in range(N_T) for n in range(N_N)]
@@ -123,32 +126,32 @@ def tile_mix_xres_tm_gelu_kernel(tc, x4_words, x4_scales, xr, w4_words, w4_scale
             first = open_bank(g)
             nc.tensor.matmul_mx(
                 out=acc[g][:],
-                lhsT=codes[i][:].bitcast(E4M3X4),
-                lhsT_scale=scales[i][:],
+                lhsT=codes[i // 2][:, i % 2 * P : i % 2 * P + P].bitcast(E4M3X4),
+                lhsT_scale=scales[i // 2][:, i % 2 * P : i % 2 * P + P],
                 rhs=w_words[:, 2 * NB * n : 2 * NB * (n + 1)].bitcast(E2M1X4),
                 rhs_scale=w_sc[:, NB * n : NB * (n + 1)],
                 start=first,
                 stop=not first,
             )
 
-        def widen(copy, n):
-            copy(out=b_wide[n][:], in_=b_cols[:, 32 * n : 32 * n + 16].unsqueeze(2).to_broadcast([P, 16, 32]))
-
-        def turn(n):
-            nc.vector.transpose(
-                out=bias[:, n * NB : (n + 1) * NB], in_=b_wide[n][:].rearrange("p j a -> p (j a)")
+        def spread_bias(n):
+            nc.vector.tensor_copy(out=b_wide[n][:], in_=b_slots[:, n, :].unsqueeze(2).to_broadcast([P, 4, P]))
+            turned = psum.tile([P, 4, P], F32, name="turned", tag="acc")
+            for c in range(4):
+                nc.tensor.transpose(turned[:, c, :], b_wide[n][:, c, :], ident[:])
+            nc.scalar.copy(
+                out=bias[:, n * NB : (n + 1) * NB].rearrange("p (k c) -> p k c", c=4),
+                in_=turned[:].rearrange("p c k -> p k c"),
             )
 
+        for n in range(N_N):
+            spread_bias(n)
         for i in range(2):
-            copy_s(i, 80, 128)
-            copy_v(i, 0, 80)
+            copy_v(i, 0, P)
         for i in range(2):
-            quantize(i)
-        nc.vector.transpose(out=b_cols[:], in_=b_rows[:])
-        widen(nc.vector.tensor_copy, 0)
-        widen(nc.scalar.copy, 1)
-        widen(nc.scalar.copy, 2)
-        turn(0)
+            quantize(0, i * P, i * P + P)
+        for j in range(2, N_T):
+            copy_g(j, 0, P)
         pass_xr(0)
         pass_xr(1)
         pass_x4(0)
@@ -156,32 +159,24 @@ def tile_mix_xres_tm_gelu_kernel(tc, x4_words, x4_scales, xr, w4_words, w4_scale
         pass_xr(2)
         pass_x4(2)
 
-        copy_slot = {2: (0, 1), 3: (0, 2)}
-        for j in range(4, N_T):
-            copy_slot[j] = (j - 3, 1)
-        quant_slot = {j: (j - 1, 0) for j in range(2, N_T)}
-
         for i in range(N_T):
             pre_t = pre.tile([P, M], F32, name="pre_t", align_bytes=64)
             res = post.tile([P, M], F32, name="res", align_bytes=64)
+            last = i == N_T - 1
             for n in range(N_N):
                 g = N_N * i + n
                 if i > 0:
                     pass_xr(g)
                 if g + LEAD < len(groups):
                     pass_x4(g + LEAD)
-                cols = slice(n * NB, (n + 1) * NB)
-                if i == 0 and n > 0:
-                    turn(n)
-                nc.vector.tensor_add(out=pre_t[:, cols], in0=acc[g][:], in1=bias[:, cols])
-                nc.scalar.activation(out=res[:, cols], in_=pre_t[:, cols], func=ACT.Gelu_apprx_tanh)
-                for j in range(2, N_T):
-                    if copy_slot[j] == (i, n):
-                        copy_v(j, 0, V_COLS)
-                        copy_s(j, V_COLS, P)
-                    if quant_slot[j] == (i, n):
-                        quantize(j)
-                if i == N_T - 1:
-                    nc.sync.dma_start(out=out[i * P : (i + 1) * P, cols], in_=res[:, cols])
-            if i < N_T - 1:
+                step = 256 if last and n == N_N - 1 else NB
+                for c in range(0, NB, step):
+                    cols = slice(n * NB + c, n * NB + c + step)
+                    nc.vector.tensor_add(out=pre_t[:, cols], in0=acc[g][:, c : c + step], in1=bias[:, cols])
+                    nc.scalar.activation(out=res[:, cols], in_=pre_t[:, cols], func=ACT.Gelu_apprx_tanh)
+                    if last:
+                        nc.sync.dma_start(out=out[i * P : (i + 1) * P, cols], in_=res[:, cols])
+                if n == 0 and i % 2 == 1 and not last:
+                    quantize((i + 1) // 2)
+            if not last:
                 nc.sync.dma_start(out=out[i * P : (i + 1) * P, :], in_=res[:])

@@ -19,8 +19,7 @@ P = 128
 NB = 512
 N_T = T // P
 N_N = M // NB
-LEAD = 3
-CHUNKS = [(0, 256), (256, 512), (768, 768)]
+CHUNKS = [(0, 128), (128, 128), (256, 256), (512, 512), (1024, 512)]
 
 
 def tile_mix_xres_tm_gelu_kernel(tc, x4_words, x4_scales, xr, w4_words, w4_scales, b, out):
@@ -28,7 +27,7 @@ def tile_mix_xres_tm_gelu_kernel(tc, x4_words, x4_scales, xr, w4_words, w4_scale
     with ExitStack() as ctx:
         keep = ctx.enter_context(tc.tile_pool(name="keep", bufs=1))
         pre = ctx.enter_context(tc.tile_pool(name="pre", bufs=3))
-        post = ctx.enter_context(tc.tile_pool(name="post", bufs=5))
+        post = ctx.enter_context(tc.tile_pool(name="post", bufs=8))
         psum = ctx.enter_context(tc.psum_pool(name="psum", bufs=8))
         ctx.enter_context(tc.manual_schedule())
 
@@ -63,7 +62,7 @@ def tile_mix_xres_tm_gelu_kernel(tc, x4_words, x4_scales, xr, w4_words, w4_scale
         for q in range(4):
             scale_dma(nc.scalar, w_sc, w4_scales, q)
         nc.scalar.activation(out=warm_out[:], in_=warm[:], func=ACT.Gelu_apprx_tanh)
-        nc.sync.dma_start(out=raw[0][:], in_=xr_rows[:, :, 0:256])
+        nc.sync.dma_start(out=raw[0][:], in_=xr_rows[:, :, 0:P])
         nc.sync.dma_start(out=w_words[:].bitcast(I32), in_=w4_words[0].bitcast(I32))
         nc.sync.dma_start(out=x_words[:].bitcast(I32), in_=x4_words[0].bitcast(I32))
         for q in range(4):
@@ -91,7 +90,7 @@ def tile_mix_xres_tm_gelu_kernel(tc, x4_words, x4_scales, xr, w4_words, w4_scale
                 out=grouped[i // 2][:, i % 2 * P + lo : i % 2 * P + hi, :], in0=src, scalar1=1.0, scalar2=0.0, op0=ALU.mult, op1=ALU.add
             )
 
-        def quantize(k, lo=0, hi=2 * P):
+        def quantize(k, lo, hi):
             nc.vector.quantize_mx(
                 out=codes[k][:, lo:hi].bitcast(E4M3X4),
                 scales=scales[k][:, lo:hi],
@@ -134,8 +133,10 @@ def tile_mix_xres_tm_gelu_kernel(tc, x4_words, x4_scales, xr, w4_words, w4_scale
                 stop=not first,
             )
 
-        def spread_bias(n):
+        def widen(n):
             nc.vector.tensor_copy(out=b_wide[n][:], in_=b_slots[:, n, :].unsqueeze(2).to_broadcast([P, 4, P]))
+
+        def spread_bias(n):
             turned = psum.tile([P, 4, P], F32, name="turned", tag="acc")
             for c in range(4):
                 nc.tensor.transpose(turned[:, c, :], b_wide[n][:, c, :], ident[:])
@@ -145,30 +146,38 @@ def tile_mix_xres_tm_gelu_kernel(tc, x4_words, x4_scales, xr, w4_words, w4_scale
             )
 
         for n in range(N_N):
-            spread_bias(n)
-        for i in range(2):
-            copy_v(i, 0, P)
-        for i in range(2):
-            quantize(0, i * P, i * P + P)
-        for j in range(2, N_T):
-            copy_g(j, 0, P)
+            widen(n)
+        copy_v(0, 0, P)
+        quantize(0, 0, P)
+        for j in range(1, N_T):
+            copy_g(j, 0, P // 2)
+            copy_g(j, P // 2, P)
+        spread_bias(0)
         pass_xr(0)
-        pass_xr(1)
+        spread_bias(1)
         pass_x4(0)
+        pass_xr(1)
         pass_x4(1)
+        spread_bias(2)
         pass_xr(2)
         pass_x4(2)
+
+        quant_after = {(0, 1): (0, P, 2 * P), (1, 1): (1, 0, P), (2, 0): (1, P, 2 * P)}
+        for k in range(2, N_T // 2):
+            quant_after[(2 * k - 1, 0)] = (k, 0, 2 * P)
 
         for i in range(N_T):
             pre_t = pre.tile([P, M], F32, name="pre_t", align_bytes=64)
             res = post.tile([P, M], F32, name="res", align_bytes=64)
             last = i == N_T - 1
+            if i > 0:
+                for n in range(N_N):
+                    pass_xr(N_N * i + n)
+            if not last:
+                for n in range(N_N):
+                    pass_x4(N_N * (i + 1) + n)
             for n in range(N_N):
                 g = N_N * i + n
-                if i > 0:
-                    pass_xr(g)
-                if g + LEAD < len(groups):
-                    pass_x4(g + LEAD)
                 step = 256 if last and n == N_N - 1 else NB
                 for c in range(0, NB, step):
                     cols = slice(n * NB + c, n * NB + c + step)
@@ -176,7 +185,7 @@ def tile_mix_xres_tm_gelu_kernel(tc, x4_words, x4_scales, xr, w4_words, w4_scale
                     nc.scalar.activation(out=res[:, cols], in_=pre_t[:, cols], func=ACT.Gelu_apprx_tanh)
                     if last:
                         nc.sync.dma_start(out=out[i * P : (i + 1) * P, cols], in_=res[:, cols])
-                if n == 0 and i % 2 == 1 and not last:
-                    quantize((i + 1) // 2)
+                if (i, n) in quant_after:
+                    quantize(*quant_after[(i, n)])
             if not last:
                 nc.sync.dma_start(out=out[i * P : (i + 1) * P, :], in_=res[:])

@@ -2,8 +2,8 @@ from contextlib import ExitStack
 
 import concourse.mybir as mybir
 
-K, M, T = 512, 1536, 1536
-FLOPS = 2 * 2 * K * M * T
+K, N, T = 512, 1536, 1536
+FLOPS = 2 * 2 * K * N * T
 
 F32 = mybir.dt.float32
 BF16 = mybir.dt.bfloat16
@@ -12,180 +12,184 @@ U32 = mybir.dt.uint32
 U8 = mybir.dt.uint8
 E4M3X4 = mybir.dt.float8_e4m3fn_x4
 E2M1X4 = mybir.dt.float4_e2m1fn_x4
-ACT = mybir.ActivationFunctionType
-ALU = mybir.AluOpType
+ADD = mybir.AluOpType.add
+MULT = mybir.AluOpType.mult
+NOT_EQUAL = mybir.AluOpType.not_equal
+GELU = mybir.ActivationFunctionType.Gelu_apprx_tanh
 
 P = 128
+J = 4
+QUADRANTS = 4
 NB = 512
-N_T = T // P
-N_N = M // NB
-CHUNKS = [(0, 128), (128, 128), (256, 256), (512, 512), (1024, 512)]
+TILES = T // P
+BANKS = N // NB
+
+XR_LOADS = [(0, 128), (128, 256), (256, 512), (512, 1024), (1024, 1536)]
+X4_FIRST = 512
+STORE_BY_BANK_FROM = 9
+LAST_PIECE = 256
 
 
 def tile_mix_xres_tm_gelu_kernel(tc, x4_words, x4_scales, xr, w4_words, w4_scales, b, out):
     nc = tc.nc
     with ExitStack() as ctx:
         keep = ctx.enter_context(tc.tile_pool(name="keep", bufs=1))
-        pre = ctx.enter_context(tc.tile_pool(name="pre", bufs=3))
-        post = ctx.enter_context(tc.tile_pool(name="post", bufs=8))
+        sums_pool = ctx.enter_context(tc.tile_pool(name="sums_pool", bufs=3))
+        result_pool = ctx.enter_context(tc.tile_pool(name="result_pool", bufs=8))
         psum = ctx.enter_context(tc.psum_pool(name="psum", bufs=8))
         ctx.enter_context(tc.manual_schedule())
 
-        w_words = keep.tile([P, 2 * M], U8, name="w_words", align_bytes=256)
-        w_sc = keep.tile([P, M], U8, name="w_sc", align_bytes=256)
-        x_words = keep.tile([P, 2 * T], U8, name="x_words", align_bytes=256)
-        x_sc = keep.tile([P, T], U8, name="x_sc", align_bytes=256)
-        b_slots = keep.tile([P, N_N, 4], F32, name="b_slots", align_bytes=64)
-        b_wide = [keep.tile([P, 4, P], F32, name="b_wide%d" % n, align_bytes=64) for n in range(N_N)]
+        w_codes = keep.tile([P, 2 * N], U8, name="w_codes", align_bytes=256)
+        w_scales = keep.tile([P, N], U8, name="w_scales", align_bytes=256)
+        x_codes = keep.tile([P, 2 * T], U8, name="x_codes", align_bytes=256)
+        x_scales = keep.tile([P, T], U8, name="x_scales", align_bytes=256)
+        xr_raw = [
+            keep.tile([P, J, hi - lo], F32, name="xr_raw%d" % i, align_bytes=256) for i, (lo, hi) in enumerate(XR_LOADS)
+        ]
+        xr_grouped = [keep.tile([P, 2 * P, J], BF16, name="xr_grouped%d" % i, align_bytes=256) for i in range(TILES // 2)]
+        xr_codes = [keep.tile([P, 2 * P], U32, name="xr_codes%d" % i, align_bytes=256) for i in range(TILES // 2)]
+        xr_scales = [keep.tile([P, 2 * P], U8, name="xr_scales%d" % i, align_bytes=64) for i in range(TILES // 2)]
+        b_slots = keep.tile([P, BANKS, 4], F32, name="b_slots", align_bytes=64)
+        b_wide = [keep.tile([P, 4, P], F32, name="b_wide%d" % w, align_bytes=64) for w in range(BANKS)]
+        bias = keep.tile([P, N], F32, name="bias", align_bytes=256)
         ident = keep.tile([P, P], F32, name="ident")
-        bias = keep.tile([P, M], F32, name="bias", align_bytes=256)
-        warm = keep.tile([P, 1], F32, name="warm")
-        warm_out = keep.tile([P, 1], F32, name="warm_out")
-        raw = [keep.tile([P, 4, w], F32, name="raw%d" % i, align_bytes=256) for i, (c, w) in enumerate(CHUNKS)]
-        grouped = [keep.tile([P, 2 * P, 4], BF16, name="grp%d" % i, align_bytes=256) for i in range(N_T // 2)]
-        codes = [keep.tile([P, 2 * P], U32, name="codes%d" % i, align_bytes=256) for i in range(N_T // 2)]
-        scales = [keep.tile([P, 2 * P], U8, name="scl%d" % i, align_bytes=64) for i in range(N_T // 2)]
+        zero = keep.tile([P, 1], F32, name="zero")
+        zero_gelu = keep.tile([P, 1], F32, name="zero_gelu")
 
-        nc.vector.memset(w_sc[:].bitcast(I32), 0)
-        nc.vector.memset(x_sc[:].bitcast(I32), 0)
-        nc.vector.memset(warm[:], 0.0)
+        nc.vector.memset(w_scales[:].bitcast(I32), 0)
+        nc.vector.memset(x_scales[:].bitcast(I32), 0)
+        nc.vector.memset(zero[:], 0.0)
         nc.vector.memset(ident[:], 0.0)
         nc.gpsimd.affine_select(
-            out=ident[:], in_=ident[:], compare_op=ALU.not_equal, fill=1.0, base=0, pattern=[[-1, P]], channel_multiplier=1
+            out=ident[:], in_=ident[:], compare_op=NOT_EQUAL, fill=1.0, base=0, pattern=[[-1, P]], channel_multiplier=1
         )
 
-        def scale_dma(eng, dst, src, q):
-            eng.dma_start(out=dst[32 * q : 32 * q + 4, :].bitcast(I32), in_=src[0][4 * q : 4 * q + 4, :].bitcast(I32))
+        def load_scales(queue, scales, source):
+            for quad in range(QUADRANTS):
+                queue.dma_start(
+                    out=scales[32 * quad : 32 * quad + 4, :].bitcast(I32),
+                    in_=source[0][4 * quad : 4 * quad + 4, :].bitcast(I32),
+                )
 
-        xr_rows = xr.rearrange("(p j) t -> p j t", j=4)
-        nc.scalar.dma_start(out=b_slots[:], in_=b.rearrange("(w p c) -> p w c", w=N_N, c=4))
-        for q in range(4):
-            scale_dma(nc.scalar, w_sc, w4_scales, q)
-        nc.scalar.activation(out=warm_out[:], in_=warm[:], func=ACT.Gelu_apprx_tanh)
-        nc.sync.dma_start(out=raw[0][:], in_=xr_rows[:, :, 0:P])
-        nc.sync.dma_start(out=w_words[:].bitcast(I32), in_=w4_words[0].bitcast(I32))
-        nc.sync.dma_start(out=x_words[:].bitcast(I32), in_=x4_words[0].bitcast(I32))
-        for q in range(4):
-            scale_dma(nc.sync, x_sc, x4_scales, q)
-        for r, (c, w) in list(zip(raw, CHUNKS))[1:]:
-            nc.sync.dma_start(out=r[:], in_=xr_rows[:, :, c : c + w])
-
-        def views(i, lo, hi):
-            t0 = i * P
-            r, c = [(r, c) for r, (c, w) in zip(raw, CHUNKS) if c <= t0 < c + w][0]
-            src = r[:, :, t0 - c + lo : t0 - c + hi].rearrange("p j (c i) -> p c j i", i=4)
-            h = i % 2 * P
-            dst = grouped[i // 2][:, h + lo : h + hi, :].rearrange("p (c i) j -> p c j i", i=4)
-            return dst, src
-
-        def copy_v(i, lo, hi):
-            dst, src = views(i, lo, hi)
-            nc.vector.tensor_copy(out=dst, in_=src)
-
-        def copy_g(i, lo, hi):
-            t0 = i * P
-            r, c = [(r, c) for r, (c, w) in zip(raw, CHUNKS) if c <= t0 < c + w][0]
-            src = r[:, :, t0 - c + lo : t0 - c + hi].rearrange("p j t -> p t j")
-            nc.gpsimd.tensor_scalar(
-                out=grouped[i // 2][:, i % 2 * P + lo : i % 2 * P + hi, :], in0=src, scalar1=1.0, scalar2=0.0, op0=ALU.mult, op1=ALU.add
+        def load_x4_codes(lo, hi):
+            nc.sync.dma_start(
+                out=x_codes[:, 2 * lo : 2 * hi].bitcast(I32), in_=x4_words[0][:, 2 * lo : 2 * hi].bitcast(I32)
             )
 
-        def quantize(k, lo, hi):
+        def load_xr(i):
+            lo, hi = XR_LOADS[i]
+            nc.sync.dma_start(out=xr_raw[i][:], in_=xr.rearrange("(p j) t -> p j t", j=J)[:, :, lo:hi])
+
+        nc.scalar.dma_start(out=b_slots[:], in_=b.rearrange("(w p c) -> p w c", w=BANKS, c=4))
+        load_scales(nc.scalar, w_scales, w4_scales)
+        load_xr(0)
+        nc.sync.dma_start(out=w_codes[:].bitcast(I32), in_=w4_words[0].bitcast(I32))
+        load_x4_codes(0, X4_FIRST)
+        load_scales(nc.sync, x_scales, x4_scales)
+        load_xr(1)
+        load_xr(2)
+        load_x4_codes(X4_FIRST, T)
+        load_xr(3)
+        load_xr(4)
+        nc.scalar.activation(out=zero_gelu[:], in_=zero[:], func=GELU)
+
+        def grouping_views(i):
+            first = i * P
+            load = [index for index, (lo, hi) in enumerate(XR_LOADS) if lo <= first < hi][0]
+            offset = first - XR_LOADS[load][0]
+            half = i % 2 * P
+            source = xr_raw[load][:, :, offset : offset + P].rearrange("p j t -> p t j")
+            return xr_grouped[i // 2][:, half : half + P, :], source
+
+        def group_on_vector(i):
+            grouped, source = grouping_views(i)
+            nc.vector.tensor_copy(out=grouped, in_=source)
+
+        def group_on_gpsimd(i):
+            grouped, source = grouping_views(i)
+            nc.gpsimd.tensor_scalar(out=grouped, in0=source, scalar1=1.0, scalar2=0.0, op0=MULT, op1=ADD)
+
+        def quantise(first, count):
+            pair, cols = first // 2, slice(first % 2 * P, (first % 2 + count) * P)
             nc.vector.quantize_mx(
-                out=codes[k][:, lo:hi].bitcast(E4M3X4),
-                scales=scales[k][:, lo:hi],
-                in_=grouped[k][:, lo:hi, :].rearrange("p t j -> p (t j)"),
+                out=xr_codes[pair][:, cols].bitcast(E4M3X4),
+                scales=xr_scales[pair][:, cols],
+                in_=xr_grouped[pair][:, cols, :].rearrange("p t j -> p (t j)"),
             )
 
-        groups = [(i, n) for i in range(N_T) for n in range(N_N)]
-        acc = {}
+        def widen_bias(w):
+            nc.vector.tensor_copy(out=b_wide[w][:], in_=b_slots[:, w, :].unsqueeze(2).to_broadcast([P, 4, P]))
 
-        def open_bank(g):
-            first = g not in acc
-            if first:
-                bank = psum.tile([P, NB], F32, name="bank", tag="acc")
-                acc[g] = bank
-            return first
-
-        def pass_x4(g):
-            i, n = groups[g]
-            first = open_bank(g)
-            nc.tensor.matmul_mx(
-                out=acc[g][:],
-                lhsT=x_words[:, 2 * P * i : 2 * P * (i + 1)].bitcast(E2M1X4),
-                lhsT_scale=x_sc[:, P * i : P * (i + 1)],
-                rhs=w_words[:, 2 * NB * n : 2 * NB * (n + 1)].bitcast(E2M1X4),
-                rhs_scale=w_sc[:, NB * n : NB * (n + 1)],
-                start=first,
-                stop=not first,
-            )
-
-        def pass_xr(g):
-            i, n = groups[g]
-            first = open_bank(g)
-            nc.tensor.matmul_mx(
-                out=acc[g][:],
-                lhsT=codes[i // 2][:, i % 2 * P : i % 2 * P + P].bitcast(E4M3X4),
-                lhsT_scale=scales[i // 2][:, i % 2 * P : i % 2 * P + P],
-                rhs=w_words[:, 2 * NB * n : 2 * NB * (n + 1)].bitcast(E2M1X4),
-                rhs_scale=w_sc[:, NB * n : NB * (n + 1)],
-                start=first,
-                stop=not first,
-            )
-
-        def widen(n):
-            nc.vector.tensor_copy(out=b_wide[n][:], in_=b_slots[:, n, :].unsqueeze(2).to_broadcast([P, 4, P]))
-
-        def spread_bias(n):
-            turned = psum.tile([P, 4, P], F32, name="turned", tag="acc")
+        def turn_bias(w):
+            turned = psum.tile([P, 4, P], F32, name="turned", tag="bank")
             for c in range(4):
-                nc.tensor.transpose(turned[:, c, :], b_wide[n][:, c, :], ident[:])
+                nc.tensor.transpose(turned[:, c, :], b_wide[w][:, c, :], ident[:])
             nc.scalar.copy(
-                out=bias[:, n * NB : (n + 1) * NB].rearrange("p (k c) -> p k c", c=4),
+                out=bias[:, w * NB : (w + 1) * NB].rearrange("p (k c) -> p k c", c=4),
                 in_=turned[:].rearrange("p c k -> p k c"),
             )
 
-        for n in range(N_N):
-            widen(n)
-        copy_v(0, 0, P)
-        quantize(0, 0, P)
-        for j in range(1, N_T):
-            copy_g(j, 0, P // 2)
-            copy_g(j, P // 2, P)
-        spread_bias(0)
-        pass_xr(0)
-        spread_bias(1)
-        pass_x4(0)
-        pass_xr(1)
-        pass_x4(1)
-        spread_bias(2)
-        pass_xr(2)
-        pass_x4(2)
+        banks = {}
 
-        quant_after = {(0, 1): (0, P, 2 * P), (1, 1): (1, 0, P), (2, 0): (1, P, 2 * P)}
-        for k in range(2, N_T // 2):
-            quant_after[(2 * k - 1, 0)] = (k, 0, 2 * P)
+        def one_pass(i, w, codes, scales):
+            first = (i, w) not in banks
+            if first:
+                bank = psum.tile([P, NB], F32, name="bank", tag="bank")
+                banks[i, w] = bank
+            nc.tensor.matmul_mx(
+                out=banks[i, w][:],
+                lhsT=codes,
+                lhsT_scale=scales,
+                rhs=w_codes[:, 2 * NB * w : 2 * NB * (w + 1)].bitcast(E2M1X4),
+                rhs_scale=w_scales[:, NB * w : NB * (w + 1)],
+                start=first,
+                stop=not first,
+            )
 
-        for i in range(N_T):
-            pre_t = pre.tile([P, M], F32, name="pre_t", align_bytes=64)
-            res = post.tile([P, M], F32, name="res", align_bytes=64)
-            last = i == N_T - 1
+        def pass_x4(i, w):
+            one_pass(i, w, x_codes[:, 2 * P * i : 2 * P * (i + 1)].bitcast(E2M1X4), x_scales[:, P * i : P * (i + 1)])
+
+        def pass_xr(i, w):
+            cols = slice(i % 2 * P, i % 2 * P + P)
+            one_pass(i, w, xr_codes[i // 2][:, cols].bitcast(E4M3X4), xr_scales[i // 2][:, cols])
+
+        for w in range(BANKS):
+            widen_bias(w)
+        group_on_vector(0)
+        quantise(0, 1)
+        for i in range(1, TILES):
+            group_on_gpsimd(i)
+        turn_bias(0)
+        turn_bias(1)
+        for w in range(BANKS):
+            if w == 2:
+                turn_bias(2)
+            pass_xr(0, w)
+            pass_x4(0, w)
+
+        quantise_behind = {(0, 1): (1, 1), (1, 1): (2, 1), (2, 0): (3, 1)}
+        for first in range(4, TILES, 2):
+            quantise_behind[first - 1, 0] = (first, 2)
+
+        for i in range(TILES):
+            rows = slice(i * P, (i + 1) * P)
+            sums = sums_pool.tile([P, N], F32, name="sums", align_bytes=64)
+            result = result_pool.tile([P, N], F32, name="result", align_bytes=64)
             if i > 0:
-                for n in range(N_N):
-                    pass_xr(N_N * i + n)
-            if not last:
-                for n in range(N_N):
-                    pass_x4(N_N * (i + 1) + n)
-            for n in range(N_N):
-                g = N_N * i + n
-                step = 256 if last and n == N_N - 1 else NB
-                for c in range(0, NB, step):
-                    cols = slice(n * NB + c, n * NB + c + step)
-                    nc.vector.tensor_add(out=pre_t[:, cols], in0=acc[g][:, c : c + step], in1=bias[:, cols])
-                    nc.scalar.activation(out=res[:, cols], in_=pre_t[:, cols], func=ACT.Gelu_apprx_tanh)
-                    if last:
-                        nc.sync.dma_start(out=out[i * P : (i + 1) * P, cols], in_=res[:, cols])
-                if (i, n) in quant_after:
-                    quantize(*quant_after[(i, n)])
-            if not last:
-                nc.sync.dma_start(out=out[i * P : (i + 1) * P, :], in_=res[:])
+                for w in range(BANKS):
+                    pass_xr(i, w)
+            if i + 1 < TILES:
+                for w in range(BANKS):
+                    pass_x4(i + 1, w)
+            for w in range(BANKS):
+                piece = LAST_PIECE if (i, w) == (TILES - 1, BANKS - 1) else NB
+                for c in range(0, NB, piece):
+                    cols = slice(w * NB + c, w * NB + c + piece)
+                    nc.vector.tensor_add(out=sums[:, cols], in0=banks[i, w][:, c : c + piece], in1=bias[:, cols])
+                    nc.scalar.activation(out=result[:, cols], in_=sums[:, cols], func=GELU)
+                    if i >= STORE_BY_BANK_FROM:
+                        nc.sync.dma_start(out=out[rows, cols], in_=result[:, cols])
+                if (i, w) in quantise_behind:
+                    quantise(*quantise_behind[i, w])
+            if i < STORE_BY_BANK_FROM:
+                nc.sync.dma_start(out=out[rows, :], in_=result[:])

from contextlib import ExitStack

import concourse.mybir as mybir

K, N, T = 512, 1536, 1536
FLOPS = 2 * 2 * K * N * T

F32 = mybir.dt.float32
BF16 = mybir.dt.bfloat16
I32 = mybir.dt.int32
U32 = mybir.dt.uint32
U8 = mybir.dt.uint8
E4M3X4 = mybir.dt.float8_e4m3fn_x4
E2M1X4 = mybir.dt.float4_e2m1fn_x4
ADD = mybir.AluOpType.add
MULT = mybir.AluOpType.mult
NOT_EQUAL = mybir.AluOpType.not_equal
GELU = mybir.ActivationFunctionType.Gelu_apprx_tanh

P = 128
J = 4
QUADRANTS = 4
NB = 512
TILES = T // P
BANKS = N // NB

XR_LOADS = [(0, 128), (128, 256), (256, 512), (512, 1024), (1024, 1536)]
X4_FIRST = 512
STORE_BY_BANK_FROM = 9
LAST_PIECE = 256


def tile_mix_xres_tm_gelu_kernel(tc, x4_words, x4_scales, xr, w4_words, w4_scales, b, out):
    nc = tc.nc
    with ExitStack() as ctx:
        keep = ctx.enter_context(tc.tile_pool(name="keep", bufs=1))
        sums_pool = ctx.enter_context(tc.tile_pool(name="sums_pool", bufs=3))
        result_pool = ctx.enter_context(tc.tile_pool(name="result_pool", bufs=8))
        psum = ctx.enter_context(tc.psum_pool(name="psum", bufs=8))
        ctx.enter_context(tc.manual_schedule())

        w_codes = keep.tile([P, 2 * N], U8, name="w_codes", align_bytes=256)
        w_scales = keep.tile([P, N], U8, name="w_scales", align_bytes=256)
        x_codes = keep.tile([P, 2 * T], U8, name="x_codes", align_bytes=256)
        x_scales = keep.tile([P, T], U8, name="x_scales", align_bytes=256)
        xr_raw = [
            keep.tile([P, J, hi - lo], F32, name="xr_raw%d" % i, align_bytes=256) for i, (lo, hi) in enumerate(XR_LOADS)
        ]
        xr_grouped = [keep.tile([P, 2 * P, J], BF16, name="xr_grouped%d" % i, align_bytes=256) for i in range(TILES // 2)]
        xr_codes = [keep.tile([P, 2 * P], U32, name="xr_codes%d" % i, align_bytes=256) for i in range(TILES // 2)]
        xr_scales = [keep.tile([P, 2 * P], U8, name="xr_scales%d" % i, align_bytes=64) for i in range(TILES // 2)]
        b_slots = keep.tile([P, BANKS, 4], F32, name="b_slots", align_bytes=64)
        b_wide = [keep.tile([P, 4, P], F32, name="b_wide%d" % w, align_bytes=64) for w in range(BANKS)]
        bias = keep.tile([P, N], F32, name="bias", align_bytes=256)
        ident = keep.tile([P, P], F32, name="ident")
        zero = keep.tile([P, 1], F32, name="zero")
        zero_gelu = keep.tile([P, 1], F32, name="zero_gelu")

        nc.vector.memset(w_scales[:].bitcast(I32), 0)
        nc.vector.memset(x_scales[:].bitcast(I32), 0)
        nc.vector.memset(zero[:], 0.0)
        nc.vector.memset(ident[:], 0.0)
        nc.gpsimd.affine_select(
            out=ident[:], in_=ident[:], compare_op=NOT_EQUAL, fill=1.0, base=0, pattern=[[-1, P]], channel_multiplier=1
        )

        def load_scales(queue, scales, source):
            for quad in range(QUADRANTS):
                queue.dma_start(
                    out=scales[32 * quad : 32 * quad + 4, :].bitcast(I32),
                    in_=source[0][4 * quad : 4 * quad + 4, :].bitcast(I32),
                )

        def load_x4_codes(lo, hi):
            nc.sync.dma_start(
                out=x_codes[:, 2 * lo : 2 * hi].bitcast(I32), in_=x4_words[0][:, 2 * lo : 2 * hi].bitcast(I32)
            )

        def load_xr(i):
            lo, hi = XR_LOADS[i]
            nc.sync.dma_start(out=xr_raw[i][:], in_=xr.rearrange("(p j) t -> p j t", j=J)[:, :, lo:hi])

        nc.scalar.dma_start(out=b_slots[:], in_=b.rearrange("(w p c) -> p w c", w=BANKS, c=4))
        load_scales(nc.scalar, w_scales, w4_scales)
        load_xr(0)
        nc.sync.dma_start(out=w_codes[:].bitcast(I32), in_=w4_words[0].bitcast(I32))
        load_x4_codes(0, X4_FIRST)
        load_scales(nc.sync, x_scales, x4_scales)
        load_xr(1)
        load_xr(2)
        load_x4_codes(X4_FIRST, T)
        load_xr(3)
        load_xr(4)
        nc.scalar.activation(out=zero_gelu[:], in_=zero[:], func=GELU)

        def grouping_views(i):
            first = i * P
            load = [index for index, (lo, hi) in enumerate(XR_LOADS) if lo <= first < hi][0]
            offset = first - XR_LOADS[load][0]
            half = i % 2 * P
            source = xr_raw[load][:, :, offset : offset + P].rearrange("p j t -> p t j")
            return xr_grouped[i // 2][:, half : half + P, :], source

        def group_on_vector(i):
            grouped, source = grouping_views(i)
            nc.vector.tensor_copy(out=grouped, in_=source)

        def group_on_gpsimd(i):
            grouped, source = grouping_views(i)
            nc.gpsimd.tensor_scalar(out=grouped, in0=source, scalar1=1.0, scalar2=0.0, op0=MULT, op1=ADD)

        def quantise(first, count):
            pair, cols = first // 2, slice(first % 2 * P, (first % 2 + count) * P)
            nc.vector.quantize_mx(
                out=xr_codes[pair][:, cols].bitcast(E4M3X4),
                scales=xr_scales[pair][:, cols],
                in_=xr_grouped[pair][:, cols, :].rearrange("p t j -> p (t j)"),
            )

        def widen_bias(w):
            nc.vector.tensor_copy(out=b_wide[w][:], in_=b_slots[:, w, :].unsqueeze(2).to_broadcast([P, 4, P]))

        def turn_bias(w):
            turned = psum.tile([P, 4, P], F32, name="turned", tag="bank")
            for c in range(4):
                nc.tensor.transpose(turned[:, c, :], b_wide[w][:, c, :], ident[:])
            nc.scalar.copy(
                out=bias[:, w * NB : (w + 1) * NB].rearrange("p (k c) -> p k c", c=4),
                in_=turned[:].rearrange("p c k -> p k c"),
            )

        banks = {}

        def one_pass(i, w, codes, scales):
            first = (i, w) not in banks
            if first:
                bank = psum.tile([P, NB], F32, name="bank", tag="bank")
                banks[i, w] = bank
            nc.tensor.matmul_mx(
                out=banks[i, w][:],
                lhsT=codes,
                lhsT_scale=scales,
                rhs=w_codes[:, 2 * NB * w : 2 * NB * (w + 1)].bitcast(E2M1X4),
                rhs_scale=w_scales[:, NB * w : NB * (w + 1)],
                start=first,
                stop=not first,
            )

        def pass_x4(i, w):
            one_pass(i, w, x_codes[:, 2 * P * i : 2 * P * (i + 1)].bitcast(E2M1X4), x_scales[:, P * i : P * (i + 1)])

        def pass_xr(i, w):
            cols = slice(i % 2 * P, i % 2 * P + P)
            one_pass(i, w, xr_codes[i // 2][:, cols].bitcast(E4M3X4), xr_scales[i // 2][:, cols])

        for w in range(BANKS):
            widen_bias(w)
        group_on_vector(0)
        quantise(0, 1)
        for i in range(1, TILES):
            group_on_gpsimd(i)
        turn_bias(0)
        turn_bias(1)
        for w in range(BANKS):
            if w == 2:
                turn_bias(2)
            pass_xr(0, w)
            pass_x4(0, w)

        quantise_behind = {(0, 1): (1, 1), (1, 1): (2, 1), (2, 0): (3, 1)}
        for first in range(4, TILES, 2):
            quantise_behind[first - 1, 0] = (first, 2)

        for i in range(TILES):
            rows = slice(i * P, (i + 1) * P)
            sums = sums_pool.tile([P, N], F32, name="sums", align_bytes=64)
            result = result_pool.tile([P, N], F32, name="result", align_bytes=64)
            if i > 0:
                for w in range(BANKS):
                    pass_xr(i, w)
            if i + 1 < TILES:
                for w in range(BANKS):
                    pass_x4(i + 1, w)
            for w in range(BANKS):
                piece = LAST_PIECE if (i, w) == (TILES - 1, BANKS - 1) else NB
                for c in range(0, NB, piece):
                    cols = slice(w * NB + c, w * NB + c + piece)
                    nc.vector.tensor_add(out=sums[:, cols], in0=banks[i, w][:, c : c + piece], in1=bias[:, cols])
                    nc.scalar.activation(out=result[:, cols], in_=sums[:, cols], func=GELU)
                    if i >= STORE_BY_BANK_FROM:
                        nc.sync.dma_start(out=out[rows, cols], in_=result[:, cols])
                if (i, w) in quantise_behind:
                    quantise(*quantise_behind[i, w])
            if i < STORE_BY_BANK_FROM:
                nc.sync.dma_start(out=out[rows, :], in_=result[:])
